import numpy as np
import ml_dtypes


def mxq(x, axis, fmt="e4m3"):
    dtype, down = {"e4m3": (ml_dtypes.float8_e4m3fn, 7), "e5m2": (ml_dtypes.float8_e5m2, 14)}[fmt]
    v = np.moveaxis(np.asarray(x, np.float32).astype(ml_dtypes.bfloat16).astype(np.float64), axis, -1)
    blocks = v.reshape(v.shape[:-1] + (-1, 32))
    amax = np.abs(blocks).max(-1, keepdims=True)
    byte = np.maximum(np.where(amax > 0, np.frexp(amax)[1] - 1 + 127, 0) - down, 1)
    scale = np.exp2(byte - 127.0)
    codes = (blocks / scale).astype(np.float32).astype(dtype).astype(np.float64)
    return np.moveaxis((codes * scale).reshape(v.shape), -1, axis)


WIDE = False


def mx_kscale(k):
    if not WIDE:
        return np.ones(k)
    levels = np.array([10, -10, 5, -5, 0])
    if k % 512:
        return np.exp2(np.random.permutation(np.resize(levels, k // 32))).repeat(32)
    a = np.empty((k // 512, 16))
    for p in range(k // 512):
        a[p, :8] = np.random.permutation(np.resize(levels, 8))
        for g in range(8):
            far = levels[np.abs(levels - a[p, g]) >= 10]
            a[p, g + 8] = far[np.random.randint(len(far))]
    return np.exp2(a.ravel()).repeat(32)


def f64(x):
    return np.asarray(x).astype(np.float64)


def striped(idx):
    return np.tile(idx.reshape(-1, 16).T, (8, 1)).astype(np.uint16)


def unstriped(offs):
    return offs[:16].T.reshape(-1).astype(np.int64)


def pack_weight(w):
    k, n = w.shape
    w = f64(np.asarray(w, np.float32).astype(ml_dtypes.bfloat16)).reshape(k // 32, 32, n)
    amax = np.abs(w).max(1)
    byte = np.clip(np.where(amax > 0, np.frexp(amax)[1] - 1 + 127 - 7, 1), 1, 254)
    scaled = (w * np.exp2(127.0 - byte)[:, None, :]).reshape(k, n).astype(np.float32)
    words = np.ascontiguousarray(scaled.reshape(k // 512, 128, 4, n).transpose(0, 1, 3, 2)).astype(ml_dtypes.float8_e4m3fn).view(np.uint8)
    return words, np.ascontiguousarray(byte.astype(np.uint8).reshape(k // 512, 16, n))


def unpack_weight(words, scales):
    g, p, n, _ = words.shape
    vals = np.ascontiguousarray(words).view(ml_dtypes.float8_e4m3fn).astype(np.float64) * np.repeat(np.exp2(scales.astype(np.float64) - 127.0), 8, axis=1)[..., None]
    return vals.transpose(0, 1, 3, 2).reshape(g * 512, n)


def sigmoid(v):
    return 1.0 / (1.0 + np.exp(-np.maximum(v, -700.0)))


K, T, S, D, N, H, V, W = 512, 4096, 1024, 4, 128, 512, 256, 2048


def setup_inputs():
    n = np.random.standard_normal
    s = mx_kscale(K)[:, None]
    u = mx_kscale(H)
    packed_xT = pack_weight(n((K, T)) * s)
    packed_eT = pack_weight(n((K, W)) * s)
    return {
        "x_words": packed_xT[0],
        "x_scales": packed_xT[1],
        "w1": (n((K, H)) / np.sqrt(K) / s).astype(np.float32),
        "e_words": packed_eT[0],
        "e_scales": packed_eT[1],
        "w2": (n((K, H)) / np.sqrt(K) / s).astype(np.float32),
        "lab": (np.random.uniform(0.0, 1.0, (H, V))).astype(np.float32),
        "unit": (np.random.uniform(0.6, 1.4, (H, 1)) * u[:, None]).astype(np.float32),
        "w3": (n((H, N)) / np.sqrt(H) / u[:, None]).astype(np.float32),
        "offs": striped(np.random.permutation(T)[:S]),
        "rstp": striped(np.random.permutation(W)[:S]),
    }


def reference(x_words, x_scales, w1, e_words, e_scales, w2, lab, unit, w3, offs, rstp):
    xq = unpack_weight(x_words, x_scales)[:, unstriped(offs)]
    y = mxq(f64(w1), 0, "e4m3").T @ xq
    e_rstp = unpack_weight(e_words, e_scales)[:, unstriped(rstp)]
    ye = mxq(f64(w2), 0, "e4m3").T @ e_rstp
    imp = 0.8 * np.tanh(y - ye)
    tot = imp.reshape(len(imp), -1, D).sum(axis=2)
    acc = sigmoid(tot)
    err = acc - f64(lab)
    two = imp + np.pad(imp, ((0, 0), (0, 1)))[:, 1:]
    dcs = np.exp(-1.0 * two)
    hid = f64(unit) * (np.repeat(err, D, axis=1) * dcs)
    return mxq(f64(w3), 0, "e4m3").T @ mxq(hid, 0, "e4m3")

@@ -1,0 +1,250 @@
+from contextlib import ExitStack
+
+import concourse.mybir as mybir
+
+K, T, W, S, D, N, H = 512, 4096, 2048, 1024, 4, 128, 512
+V = S // D
+FLOPS = 2 * (2 * K * H * S + H * N * S)
+
+F32 = mybir.dt.float32
+BF16 = mybir.dt.bfloat16
+I32 = mybir.dt.int32
+U32 = mybir.dt.uint32
+U16 = mybir.dt.uint16
+U8 = mybir.dt.uint8
+FP8X4 = mybir.dt.float8_e4m3fn_x4
+ACT = mybir.ActivationFunctionType
+ALU = mybir.AluOpType
+
+P = 128
+PACK = 4
+BANK_STEPS = 128
+BANKS = S // BANK_STEPS
+X_SLICE = 512
+E_SLICE = 256
+CHUNK_BANKS = (1, 2, 2, 2, 1)
+DIFF_BANKS = 3
+OUT_BANKS = 4
+
+
+def tile_picked_yprimr_exp_p_kernel(
+    tc, x_words, x_scales, w1, e_words, e_scales, w2, lab, unit, w3, offs, rstp, out
+):
+    nc = tc.nc
+    with ExitStack() as ctx:
+        keep = ctx.enter_context(tc.tile_pool(name="keep", bufs=1))
+        psum = ctx.enter_context(tc.psum_pool(name="psum", bufs=1))
+
+        def sb(shape, dtype, name, tag=None):
+            return keep.tile(shape, dtype, name=name, tag=tag or name, align_bytes=64)
+
+        x_list = sb([P, S // 16], U16, "x_list")
+        e_list = sb([P, S // 16], U16, "e_list")
+        x_table = sb([P, T], U32, "x_table")
+        e_table = sb([P, W], U32, "e_table")
+        x_scale_table = sb([P, T], U8, "x_scale_table")
+        e_scale_table = sb([P, W], U8, "e_scale_table")
+        w1_raw = sb([P, PACK * H], F32, "w1_raw")
+        w2_raw = sb([P, PACK * H], F32, "w2_raw")
+        w3_raw = sb([P, PACK * N], F32, "w3_raw")
+        lab_raw = sb([P, PACK * V], F32, "lab_raw")
+        unit_sb = sb([P, PACK], F32, "unit_sb")
+
+        nc.gpsimd.memset(e_scale_table[:].bitcast(I32), 0)
+        nc.vector.memset(x_scale_table[:].bitcast(I32), 0)
+        w1_rows = w1.rearrange("(p j) c -> p (j c)", j=PACK)
+        nc.sync.dma_start(x_list[:], offs)
+        nc.sync.dma_start(w1_raw[:, : 2 * H], w1_rows[:, : 2 * H])
+        nc.sync.dma_start(e_list[:], rstp)
+        nc.sync.dma_start(w1_raw[:, 2 * H :], w1_rows[:, 2 * H :])
+        for r in range(4):
+            nc.sync.dma_start(e_scale_table[r:P:32, :].bitcast(I32), e_scales[0][r:16:4, :].bitcast(I32))
+        nc.sync.dma_start(w2_raw[:], w2.rearrange("(p j) c -> p (j c)", j=PACK))
+        for r in range(4):
+            nc.sync.dma_start(x_scale_table[r:P:32, :].bitcast(I32), x_scales[0][r:16:4, :].bitcast(I32))
+        nc.sync.dma_start(x_table[:].bitcast(I32), x_words[0].rearrange("p n r -> p (n r)").bitcast(I32))
+        nc.sync.dma_start(e_table[:].bitcast(I32), e_words[0].rearrange("p n r -> p (n r)").bitcast(I32))
+        nc.sync.dma_start(lab_raw[:], lab.rearrange("(p t) v -> p (t v)", t=PACK))
+        nc.sync.dma_start(unit_sb[:], unit.rearrange("(p t) o -> p (t o)", t=PACK))
+        nc.sync.dma_start(w3_raw[:], w3.rearrange("(p t) m -> p (t m)", t=PACK))
+
+        e_scale = sb([P, S], U8, "e_scale")
+        nc.vector.tensor_copy(e_scale[:], e_scale_table[:].indirect(e_list[:]))
+        x_scale = sb([P, S], U8, "x_scale")
+        nc.vector.tensor_copy(x_scale[:], x_scale_table[:].indirect(x_list[:]))
+
+        w_scales = sb([P, 2 * H], U8, "w_scales", "x_scale_table")
+
+        def quantise_first(raw, sign, name, scale):
+            dealt = sb([P, PACK * H], BF16, name + "_dealt")
+            nc.scalar.activation(
+                dealt[:].rearrange("p (t m j) -> p m t j", t=PACK, j=PACK),
+                raw[:].rearrange("p (j m t) -> p m t j", j=PACK, t=PACK),
+                ACT.Copy,
+                scale=sign,
+            )
+            codes = sb([P, H], U32, name + "_codes")
+            nc.vector.quantize_mx(codes[:].bitcast(FP8X4), scale, dealt[:])
+            return codes
+
+        w1_scale, w2_scale = w_scales[:, :H], w_scales[:, H:]
+        w1_codes = quantise_first(w1_raw, 1.0, "w1", w1_scale)
+        w2_codes = quantise_first(w2_raw, -1.0, "w2", w2_scale)
+
+        diff = {}
+
+        def first_product(bank, w_codes, w_scale, codes, col0, scale, opens):
+            steps = slice(bank * BANK_STEPS, (bank + 1) * BANK_STEPS)
+            local = slice(steps.start - col0, steps.stop - col0)
+            for t in range(PACK):
+                cols = slice(t * P, (t + 1) * P)
+                nc.tensor.matmul_mx(
+                    diff[bank][:, t * BANK_STEPS : (t + 1) * BANK_STEPS],
+                    lhsT=w_codes[:, cols].bitcast(FP8X4),
+                    lhsT_scale=w_scale[:, cols],
+                    rhs=codes[:, local].bitcast(FP8X4),
+                    rhs_scale=scale[:, steps],
+                    start=(opens and t == 0),
+                    stop=(not opens and t == PACK - 1),
+                )
+
+        x_codes = []
+        for s0 in range(0, S, X_SLICE):
+            picked = sb([P, X_SLICE], U32, "x_codes%d" % s0, "w2_dealt" if s0 == 0 else None)
+            nc.vector.tensor_copy(picked[:], x_table[:].indirect(x_list[:, s0 // 16 : (s0 + X_SLICE) // 16]))
+            x_codes.append(picked)
+        e_codes = []
+        for s0 in range(0, S, E_SLICE):
+            picked = sb([P, E_SLICE], U32, "e_codes%d" % s0)
+            nc.vector.tensor_copy(picked[:], e_table[:].indirect(e_list[:, s0 // 16 : (s0 + E_SLICE) // 16]))
+            e_codes.append(picked)
+
+        th = sb([P, (S + 1) * PACK], F32, "th")
+        nc.gpsimd.memset(th[:, S * PACK :], 0.0)
+
+        def x_product(b):
+            diff[b] = psum.tile([P, PACK * BANK_STEPS], F32, name="diff%d" % b, tag="diff%d" % (b % DIFF_BANKS))
+            i = b * BANK_STEPS // X_SLICE
+            first_product(b, w1_codes, w1_scale, x_codes[i], i * X_SLICE, x_scale, True)
+
+        for b in range(DIFF_BANKS):
+            x_product(b)
+
+        def tanh_bank(b):
+            i = b * BANK_STEPS // E_SLICE
+            first_product(b, w2_codes, w2_scale, e_codes[i], i * E_SLICE, e_scale, False)
+            nc.scalar.activation(
+                th[:, b * BANK_STEPS * PACK : (b + 1) * BANK_STEPS * PACK].rearrange("p (s t) -> p s t", t=PACK),
+                diff[b][:].rearrange("p (t s) -> p s t", t=PACK),
+                ACT.Tanh,
+            )
+            if b + DIFF_BANKS < BANKS:
+                x_product(b + DIFF_BANKS)
+
+        starts = [sum(CHUNK_BANKS[:c]) * BANK_STEPS for c in range(len(CHUNK_BANKS))]
+        widths = [nb * BANK_STEPS for nb in CHUNK_BANKS]
+        nchunks = len(CHUNK_BANKS)
+        two = [sb([P, n * PACK], F32, "two%d" % c) for c, n in enumerate(widths)]
+        dcs = [sb([P, n * PACK], F32, "dcs%d" % c) for c, n in enumerate(widths)]
+        tot = [sb([P, n], F32, "tot%d" % c) for c, n in enumerate(widths)]
+        half = [sb([P, n], F32, "half%d" % c) for c, n in enumerate(widths)]
+        rest = [sb([P, n], F32, "rest%d" % c) for c, n in enumerate(widths)]
+        err = [sb([P, n], F32, "err%d" % c) for c, n in enumerate(widths)]
+        erru = [sb([P, n], F32, "erru%d" % c) for c, n in enumerate(widths)]
+        hid = [sb([P, n * PACK], BF16, "hid%d" % c) for c, n in enumerate(widths)]
+        hid_codes = [sb([P, n], U32, "hid_codes%d" % c) for c, n in enumerate(widths)]
+        hid_scale = [sb([P, n], U8, "hid_scale%d" % c) for c, n in enumerate(widths)]
+
+        def pair_sums(c):
+            a, n = starts[c] * PACK, widths[c] * PACK
+            nc.vector.tensor_tensor(two[c][:], th[:, a : a + n], th[:, a + PACK : a + n + PACK], ALU.add)
+
+        def totals(c):
+            pairs = two[c][:].rearrange("p (v d t) -> p v d t", d=D, t=PACK)
+            nc.vector.tensor_tensor(
+                tot[c][:].rearrange("p (v t) -> p v t", t=PACK), pairs[:, :, 0, :], pairs[:, :, 2, :], ALU.add
+            )
+
+        def scalar_stage(c):
+            v0, nv = starts[c] // D, widths[c] // D
+            nc.scalar.activation(dcs[c][:], two[c][:], ACT.Exp, scale=-0.8)
+            nc.scalar.activation(half[c][:], tot[c][:], ACT.Tanh, scale=0.4)
+            nc.scalar.activation(
+                rest[c][:].rearrange("p (v t) -> p v t", t=PACK),
+                lab_raw[:].rearrange("p (t v) -> p v t", t=PACK)[:, v0 : v0 + nv, :],
+                ACT.Copy,
+                scale=-1.0,
+                bias=0.5,
+            )
+
+        def errors(c):
+            nc.vector.scalar_tensor_tensor(err[c][:], half[c][:], 0.5, rest[c][:], ALU.mult, ALU.add)
+
+        def scaled_errors(c):
+            nv = widths[c] // D
+            nc.vector.tensor_tensor(
+                erru[c][:].rearrange("p (v t) -> p v t", t=PACK),
+                err[c][:].rearrange("p (v t) -> p v t", t=PACK),
+                unit_sb[:].unsqueeze(1).to_broadcast([P, nv, PACK]),
+                ALU.mult,
+            )
+
+        def hidden(c):
+            nv = widths[c] // D
+            nc.vector.tensor_tensor(
+                hid[c][:].rearrange("p (v d t) -> p v d t", d=D, t=PACK),
+                dcs[c][:].rearrange("p (v d t) -> p v d t", d=D, t=PACK),
+                erru[c][:].rearrange("p (v t) -> p v t", t=PACK).unsqueeze(2).to_broadcast([P, nv, D, PACK]),
+                ALU.mult,
+            )
+
+        w3_grouped = sb([P, PACK * N], BF16, "w3_grouped")
+        w3_codes = sb([P, N], U32, "w3_codes")
+        w3_scale = sb([P, N], U8, "w3_scale")
+
+        def quantise_w3():
+            nc.scalar.activation(
+                w3_grouped[:].rearrange("p (m t) -> p m t", t=PACK),
+                w3_raw[:].rearrange("p (t m) -> p m t", t=PACK),
+                ACT.Copy,
+            )
+            nc.vector.quantize_mx(w3_codes[:].bitcast(FP8X4), w3_scale[:], w3_grouped[:])
+
+        def finish(c):
+            n = widths[c]
+            nc.vector.quantize_mx(hid_codes[c][:].bitcast(FP8X4), hid_scale[c][:], hid[c][:])
+            acc = psum.tile([P, PACK * BANK_STEPS], F32, name="acc%d" % c, tag="acc%d" % (c % OUT_BANKS))
+            nc.tensor.matmul_mx(
+                acc[:, :n],
+                lhsT=w3_codes[:].bitcast(FP8X4),
+                lhsT_scale=w3_scale[:],
+                rhs=hid_codes[c][:].bitcast(FP8X4),
+                rhs_scale=hid_scale[c][:],
+                start=True,
+                stop=True,
+            )
+            res = sb([P, n], F32, "res%d" % c)
+            nc.scalar.copy(res[:], acc[:, :n])
+            nc.sync.dma_start(out[:, starts[c] : starts[c] + n], res[:])
+
+        done_banks = 0
+        for r in range(nchunks + 2):
+            if r < nchunks:
+                need = min(BANKS, (starts[r] + widths[r]) // BANK_STEPS + 1)
+                for b in range(done_banks, need):
+                    tanh_bank(b)
+                done_banks = need
+                pair_sums(r)
+            if 1 <= r <= nchunks:
+                errors(r - 1)
+            if r < nchunks:
+                totals(r)
+                scalar_stage(r)
+            if r == 1:
+                quantise_w3()
+            if 1 <= r <= nchunks:
+                scaled_errors(r - 1)
+            if r >= 2:
+                finish(r - 2)
+            if 1 <= r <= nchunks:
+                hidden(r - 1)

@@ -20,6 +20,7 @@ P = 128
 PACK = 4
 BANK_STEPS = 128
 BANKS = S // BANK_STEPS
+E_ROW = 4
 X_SLICE = 512
 E_SLICE = 256
 CHUNK_BANKS = (1, 2, 2, 2, 1)
@@ -50,15 +51,20 @@ def tile_picked_yprimr_exp_p_kernel(
         lab_raw = sb([P, PACK * V], F32, "lab_raw")
         unit_sb = sb([P, PACK], F32, "unit_sb")
 
+        th = sb([P, (S + 1) * PACK], F32, "th")
+        past_end = sb([P, PACK], F32, "past_end")
+
         nc.gpsimd.memset(e_scale_table[:].bitcast(I32), 0)
         nc.vector.memset(x_scale_table[:].bitcast(I32), 0)
+        nc.gpsimd.memset(past_end[:], 0.0)
+        nc.scalar.activation(th[:, S * PACK :], past_end[:], ACT.Tanh)
         w1_rows = w1.rearrange("(p j) c -> p (j c)", j=PACK)
         nc.sync.dma_start(x_list[:], offs)
         nc.sync.dma_start(w1_raw[:, : 2 * H], w1_rows[:, : 2 * H])
         nc.sync.dma_start(e_list[:], rstp)
         nc.sync.dma_start(w1_raw[:, 2 * H :], w1_rows[:, 2 * H :])
         for r in range(4):
-            nc.sync.dma_start(e_scale_table[r:P:32, :].bitcast(I32), e_scales[0][r:16:4, :].bitcast(I32))
+            nc.sync.dma_start(e_scale_table[E_ROW + r : P : 32, :].bitcast(I32), e_scales[0][r:16:4, :].bitcast(I32))
         nc.sync.dma_start(w2_raw[:], w2.rearrange("(p j) c -> p (j c)", j=PACK))
         for r in range(4):
             nc.sync.dma_start(x_scale_table[r:P:32, :].bitcast(I32), x_scales[0][r:16:4, :].bitcast(I32))
@@ -119,8 +125,6 @@ def tile_picked_yprimr_exp_p_kernel(
             nc.vector.tensor_copy(picked[:], e_table[:].indirect(e_list[:, s0 // 16 : (s0 + E_SLICE) // 16]))
             e_codes.append(picked)
 
-        th = sb([P, (S + 1) * PACK], F32, "th")
-        nc.gpsimd.memset(th[:, S * PACK :], 0.0)
 
         def x_product(b):
             diff[b] = psum.tile([P, PACK * BANK_STEPS], F32, name="diff%d" % b, tag="diff%d" % (b % DIFF_BANKS))
@@ -132,7 +136,7 @@ def tile_picked_yprimr_exp_p_kernel(
 
         def tanh_bank(b):
             i = b * BANK_STEPS // E_SLICE
-            first_product(b, w2_codes, w2_scale, e_codes[i], i * E_SLICE, e_scale, False)
+            first_product(b, w2_codes, w2_scale, e_codes[i], i * E_SLICE, e_scale[E_ROW:, :], False)
             nc.scalar.activation(
                 th[:, b * BANK_STEPS * PACK : (b + 1) * BANK_STEPS * PACK].rearrange("p (s t) -> p s t", t=PACK),
                 diff[b][:].rearrange("p (t s) -> p s t", t=PACK),
@@ -144,8 +148,9 @@ def tile_picked_yprimr_exp_p_kernel(
         starts = [sum(CHUNK_BANKS[:c]) * BANK_STEPS for c in range(len(CHUNK_BANKS))]
         widths = [nb * BANK_STEPS for nb in CHUNK_BANKS]
         nchunks = len(CHUNK_BANKS)
-        two = [sb([P, n * PACK], F32, "two%d" % c) for c, n in enumerate(widths)]
-        dcs = [sb([P, n * PACK], F32, "dcs%d" % c) for c, n in enumerate(widths)]
+        two = sb([P, S * PACK], F32, "two")
+        dcs = sb([P, S * PACK], F32, "dcs")
+        edges = [0] + [s - 1 for s in starts[1:]] + [S]
         tot = [sb([P, n], F32, "tot%d" % c) for c, n in enumerate(widths)]
         half = [sb([P, n], F32, "half%d" % c) for c, n in enumerate(widths)]
         rest = [sb([P, n], F32, "rest%d" % c) for c, n in enumerate(widths)]
@@ -156,19 +161,25 @@ def tile_picked_yprimr_exp_p_kernel(
         hid_scale = [sb([P, n], U8, "hid_scale%d" % c) for c, n in enumerate(widths)]
 
         def pair_sums(c):
-            a, n = starts[c] * PACK, widths[c] * PACK
-            nc.vector.tensor_tensor(two[c][:], th[:, a : a + n], th[:, a + PACK : a + n + PACK], ALU.add)
+            a, b = edges[c] * PACK, edges[c + 1] * PACK
+            nc.vector.tensor_tensor(two[:, a:b], th[:, a:b], th[:, a + PACK : b + PACK], ALU.add)
+
+        def steps_of(tile, c):
+            return tile[:, starts[c] * PACK : (starts[c] + widths[c]) * PACK].rearrange("p (v d t) -> p v d t", d=D, t=PACK)
 
         def totals(c):
-            pairs = two[c][:].rearrange("p (v d t) -> p v d t", d=D, t=PACK)
+            pairs = steps_of(two, c)
             nc.vector.tensor_tensor(
                 tot[c][:].rearrange("p (v t) -> p v t", t=PACK), pairs[:, :, 0, :], pairs[:, :, 2, :], ALU.add
             )
-
-        def scalar_stage(c):
-            v0, nv = starts[c] // D, widths[c] // D
-            nc.scalar.activation(dcs[c][:], two[c][:], ACT.Exp, scale=-0.8)
             nc.scalar.activation(half[c][:], tot[c][:], ACT.Tanh, scale=0.4)
+
+        def discounts(c):
+            a, b = edges[c] * PACK, edges[c + 1] * PACK
+            nc.scalar.activation(dcs[:, a:b], two[:, a:b], ACT.Exp, scale=-0.8)
+
+        def outcomes(c):
+            v0, nv = starts[c] // D, widths[c] // D
             nc.scalar.activation(
                 rest[c][:].rearrange("p (v t) -> p v t", t=PACK),
                 lab_raw[:].rearrange("p (t v) -> p v t", t=PACK)[:, v0 : v0 + nv, :],
@@ -193,7 +204,7 @@ def tile_picked_yprimr_exp_p_kernel(
             nv = widths[c] // D
             nc.vector.tensor_tensor(
                 hid[c][:].rearrange("p (v d t) -> p v d t", d=D, t=PACK),
-                dcs[c][:].rearrange("p (v d t) -> p v d t", d=D, t=PACK),
+                steps_of(dcs, c),
                 erru[c][:].rearrange("p (v t) -> p v t", t=PACK).unsqueeze(2).to_broadcast([P, nv, D, PACK]),
                 ALU.mult,
             )
@@ -227,24 +238,27 @@ def tile_picked_yprimr_exp_p_kernel(
             nc.scalar.copy(res[:], acc[:, :n])
             nc.sync.dma_start(out[:, starts[c] : starts[c] + n], res[:])
 
-        done_banks = 0
+        def tanh_chunk(c):
+            for b in range(starts[c] // BANK_STEPS, (starts[c] + widths[c]) // BANK_STEPS):
+                tanh_bank(b)
+
+        tanh_chunk(0)
         for r in range(nchunks + 2):
             if r < nchunks:
-                need = min(BANKS, (starts[r] + widths[r]) // BANK_STEPS + 1)
-                for b in range(done_banks, need):
-                    tanh_bank(b)
-                done_banks = need
                 pair_sums(r)
+            if r + 1 < nchunks:
+                tanh_chunk(r + 1)
             if 1 <= r <= nchunks:
                 errors(r - 1)
             if r < nchunks:
                 totals(r)
-                scalar_stage(r)
+                outcomes(r)
+                discounts(r)
             if r == 1:
                 quantise_w3()
+            if r >= 2:
+                hidden(r - 2)
             if 1 <= r <= nchunks:
                 scaled_errors(r - 1)
             if r >= 2:
                 finish(r - 2)
-            if 1 <= r <= nchunks:
-                hidden(r - 1)

@@ -21,11 +21,8 @@ PACK = 4
 BANK_STEPS = 128
 BANKS = S // BANK_STEPS
 E_ROW = 4
-X_SLICE = 512
-E_SLICE = 256
+SLICE = 512
 CHUNK_BANKS = (1, 2, 2, 2, 1)
-DIFF_BANKS = 3
-OUT_BANKS = 4
 
 
 def tile_picked_yprimr_exp_p_kernel(
@@ -58,46 +55,59 @@ def tile_picked_yprimr_exp_p_kernel(
         nc.vector.memset(x_scale_table[:].bitcast(I32), 0)
         nc.gpsimd.memset(past_end[:], 0.0)
         nc.scalar.activation(th[:, S * PACK :], past_end[:], ACT.Tanh)
-        w1_rows = w1.rearrange("(p j) c -> p (j c)", j=PACK)
-        nc.sync.dma_start(x_list[:], offs)
-        nc.sync.dma_start(w1_raw[:, : 2 * H], w1_rows[:, : 2 * H])
+        w2_rows = w2.rearrange("(p j) c -> p (j c)", j=PACK)
         nc.sync.dma_start(e_list[:], rstp)
-        nc.sync.dma_start(w1_raw[:, 2 * H :], w1_rows[:, 2 * H :])
+        nc.sync.dma_start(w2_raw[:, : 2 * H], w2_rows[:, : 2 * H])
+        nc.sync.dma_start(x_list[:], offs)
+        nc.sync.dma_start(w2_raw[:, 2 * H :], w2_rows[:, 2 * H :])
         for r in range(4):
             nc.sync.dma_start(e_scale_table[E_ROW + r : P : 32, :].bitcast(I32), e_scales[0][r:16:4, :].bitcast(I32))
-        nc.sync.dma_start(w2_raw[:], w2.rearrange("(p j) c -> p (j c)", j=PACK))
+        nc.sync.dma_start(w1_raw[:], w1.rearrange("(p j) c -> p (j c)", j=PACK))
         for r in range(4):
             nc.sync.dma_start(x_scale_table[r:P:32, :].bitcast(I32), x_scales[0][r:16:4, :].bitcast(I32))
-        nc.sync.dma_start(x_table[:].bitcast(I32), x_words[0].rearrange("p n r -> p (n r)").bitcast(I32))
         nc.sync.dma_start(e_table[:].bitcast(I32), e_words[0].rearrange("p n r -> p (n r)").bitcast(I32))
+        nc.sync.dma_start(x_table[:].bitcast(I32), x_words[0].rearrange("p n r -> p (n r)").bitcast(I32))
         nc.sync.dma_start(lab_raw[:], lab.rearrange("(p t) v -> p (t v)", t=PACK))
         nc.sync.dma_start(unit_sb[:], unit.rearrange("(p t) o -> p (t o)", t=PACK))
         nc.sync.dma_start(w3_raw[:], w3.rearrange("(p t) m -> p (t m)", t=PACK))
 
-        e_scale = sb([P, S], U8, "e_scale")
-        nc.vector.tensor_copy(e_scale[:], e_scale_table[:].indirect(e_list[:]))
-        x_scale = sb([P, S], U8, "x_scale")
-        nc.vector.tensor_copy(x_scale[:], x_scale_table[:].indirect(x_list[:]))
-
-        w_scales = sb([P, 2 * H], U8, "w_scales", "x_scale_table")
-
-        def quantise_first(raw, sign, name, scale):
-            dealt = sb([P, PACK * H], BF16, name + "_dealt")
+        def deal(raw, sign, name):
+            dealt = sb([P, PACK * H], BF16, name)
             nc.scalar.activation(
                 dealt[:].rearrange("p (t m j) -> p m t j", t=PACK, j=PACK),
                 raw[:].rearrange("p (j m t) -> p m t j", j=PACK, t=PACK),
                 ACT.Copy,
                 scale=sign,
             )
-            codes = sb([P, H], U32, name + "_codes")
-            nc.vector.quantize_mx(codes[:].bitcast(FP8X4), scale, dealt[:])
-            return codes
+            return dealt
 
-        w1_scale, w2_scale = w_scales[:, :H], w_scales[:, H:]
-        w1_codes = quantise_first(w1_raw, 1.0, "w1", w1_scale)
-        w2_codes = quantise_first(w2_raw, -1.0, "w2", w2_scale)
+        def quantise(dealt, name, tag):
+            codes = sb([P, H], U32, name + "_codes", tag)
+            scale = sb([P, H], U8, name + "_scale")
+            nc.vector.quantize_mx(codes[:].bitcast(FP8X4), scale[:], dealt[:])
+            return codes, scale
 
-        diff = {}
+        def gather_words(table, entries, name, first_tag):
+            pieces = []
+            for s0 in range(0, S, SLICE):
+                picked = sb([P, SLICE], U32, name + str(s0), first_tag if s0 == 0 else None)
+                nc.vector.tensor_copy(picked[:], table[:].indirect(entries[:, s0 // 16 : (s0 + SLICE) // 16]))
+                pieces.append(picked)
+            return pieces
+
+        w2_dealt = deal(w2_raw, -1.0, "w2_dealt")
+        w1_dealt = deal(w1_raw, 1.0, "w1_dealt")
+
+        e_scale = sb([P, S], U8, "e_scale")
+        nc.vector.tensor_copy(e_scale[:], e_scale_table[:].indirect(e_list[:]))
+        w2_codes, w2_scale = quantise(w2_dealt, "w2", "e_scale_table")
+        x_scale = sb([P, S], U8, "x_scale")
+        nc.vector.tensor_copy(x_scale[:], x_scale_table[:].indirect(x_list[:]))
+        e_codes = gather_words(e_table, e_list, "e_codes", "x_scale_table")
+        w1_codes, w1_scale = quantise(w1_dealt, "w1", "e_table")
+        x_codes = gather_words(x_table, x_list, "x_codes", "w1_dealt")
+
+        diff = [psum.tile([P, PACK * BANK_STEPS], F32, name="diff%d" % b, tag="bank%d" % b) for b in range(BANKS)]
 
         def first_product(bank, w_codes, w_scale, codes, col0, scale, opens):
             steps = slice(bank * BANK_STEPS, (bank + 1) * BANK_STEPS)
@@ -114,36 +124,18 @@ def tile_picked_yprimr_exp_p_kernel(
                     stop=(not opens and t == PACK - 1),
                 )
 
-        x_codes = []
-        for s0 in range(0, S, X_SLICE):
-            picked = sb([P, X_SLICE], U32, "x_codes%d" % s0, "w2_dealt" if s0 == 0 else None)
-            nc.vector.tensor_copy(picked[:], x_table[:].indirect(x_list[:, s0 // 16 : (s0 + X_SLICE) // 16]))
-            x_codes.append(picked)
-        e_codes = []
-        for s0 in range(0, S, E_SLICE):
-            picked = sb([P, E_SLICE], U32, "e_codes%d" % s0)
-            nc.vector.tensor_copy(picked[:], e_table[:].indirect(e_list[:, s0 // 16 : (s0 + E_SLICE) // 16]))
-            e_codes.append(picked)
-
-
-        def x_product(b):
-            diff[b] = psum.tile([P, PACK * BANK_STEPS], F32, name="diff%d" % b, tag="diff%d" % (b % DIFF_BANKS))
-            i = b * BANK_STEPS // X_SLICE
-            first_product(b, w1_codes, w1_scale, x_codes[i], i * X_SLICE, x_scale, True)
-
-        for b in range(DIFF_BANKS):
-            x_product(b)
+        for b in range(BANKS):
+            i = b * BANK_STEPS // SLICE
+            first_product(b, w2_codes, w2_scale, e_codes[i], i * SLICE, e_scale[E_ROW:, :], True)
 
         def tanh_bank(b):
-            i = b * BANK_STEPS // E_SLICE
-            first_product(b, w2_codes, w2_scale, e_codes[i], i * E_SLICE, e_scale[E_ROW:, :], False)
+            i = b * BANK_STEPS // SLICE
+            first_product(b, w1_codes, w1_scale, x_codes[i], i * SLICE, x_scale, False)
             nc.scalar.activation(
                 th[:, b * BANK_STEPS * PACK : (b + 1) * BANK_STEPS * PACK].rearrange("p (s t) -> p s t", t=PACK),
                 diff[b][:].rearrange("p (t s) -> p s t", t=PACK),
                 ACT.Tanh,
             )
-            if b + DIFF_BANKS < BANKS:
-                x_product(b + DIFF_BANKS)
 
         starts = [sum(CHUNK_BANKS[:c]) * BANK_STEPS for c in range(len(CHUNK_BANKS))]
         widths = [nb * BANK_STEPS for nb in CHUNK_BANKS]
@@ -224,7 +216,7 @@ def tile_picked_yprimr_exp_p_kernel(
         def finish(c):
             n = widths[c]
             nc.vector.quantize_mx(hid_codes[c][:].bitcast(FP8X4), hid_scale[c][:], hid[c][:])
-            acc = psum.tile([P, PACK * BANK_STEPS], F32, name="acc%d" % c, tag="acc%d" % (c % OUT_BANKS))
+            acc = psum.tile([P, PACK * BANK_STEPS], F32, name="acc%d" % c, tag="bank%d" % c)
             nc.tensor.matmul_mx(
                 acc[:, :n],
                 lhsT=w3_codes[:].bitcast(FP8X4),

@@ -20,9 +20,10 @@ P = 128
 PACK = 4
 BANK_STEPS = 128
 BANKS = S // BANK_STEPS
-E_ROW = 4
+X_ROW = 8
+SPREAD_FIRST, SPREAD_STEP = 4, 8
 SLICE = 512
-CHUNK_BANKS = (1, 2, 2, 2, 1)
+CHUNK = 256
 
 
 def tile_picked_yprimr_exp_p_kernel(
@@ -54,6 +55,8 @@ def tile_picked_yprimr_exp_p_kernel(
         nc.gpsimd.memset(e_scale_table[:].bitcast(I32), 0)
         nc.vector.memset(x_scale_table[:].bitcast(I32), 0)
         nc.gpsimd.memset(past_end[:], 0.0)
+        x_scale = sb([P, S], U8, "x_scale")
+        nc.gpsimd.memset(x_scale[:].bitcast(I32), 0)
         nc.scalar.activation(th[:, S * PACK :], past_end[:], ACT.Tanh)
         w2_rows = w2.rearrange("(p j) c -> p (j c)", j=PACK)
         nc.sync.dma_start(e_list[:], rstp)
@@ -61,10 +64,9 @@ def tile_picked_yprimr_exp_p_kernel(
         nc.sync.dma_start(x_list[:], offs)
         nc.sync.dma_start(w2_raw[:, 2 * H :], w2_rows[:, 2 * H :])
         for r in range(4):
-            nc.sync.dma_start(e_scale_table[E_ROW + r : P : 32, :].bitcast(I32), e_scales[0][r:16:4, :].bitcast(I32))
+            nc.sync.dma_start(e_scale_table[r:P:32, :].bitcast(I32), e_scales[0][r:16:4, :].bitcast(I32))
         nc.sync.dma_start(w1_raw[:], w1.rearrange("(p j) c -> p (j c)", j=PACK))
-        for r in range(4):
-            nc.sync.dma_start(x_scale_table[r:P:32, :].bitcast(I32), x_scales[0][r:16:4, :].bitcast(I32))
+        nc.sync.dma_start(x_scale_table[SPREAD_FIRST:P:SPREAD_STEP, :].bitcast(I32), x_scales[0].bitcast(I32))
         nc.sync.dma_start(e_table[:].bitcast(I32), e_words[0].rearrange("p n r -> p (n r)").bitcast(I32))
         nc.sync.dma_start(x_table[:].bitcast(I32), x_words[0].rearrange("p n r -> p (n r)").bitcast(I32))
         nc.sync.dma_start(lab_raw[:], lab.rearrange("(p t) v -> p (t v)", t=PACK))
@@ -100,10 +102,15 @@ def tile_picked_yprimr_exp_p_kernel(
 
         e_scale = sb([P, S], U8, "e_scale")
         nc.vector.tensor_copy(e_scale[:], e_scale_table[:].indirect(e_list[:]))
-        w2_codes, w2_scale = quantise(w2_dealt, "w2", "e_scale_table")
-        x_scale = sb([P, S], U8, "x_scale")
-        nc.vector.tensor_copy(x_scale[:], x_scale_table[:].indirect(x_list[:]))
-        e_codes = gather_words(e_table, e_list, "e_codes", "x_scale_table")
+        x_spread = sb([P, S], U8, "x_spread", "e_scale_table")
+        nc.vector.tensor_copy(x_spread[:], x_scale_table[:].indirect(x_list[:]))
+        for r in range(4):
+            nc.scalar.dma_start(
+                x_scale[X_ROW + r : P : 32, :].bitcast(I32),
+                x_spread[SPREAD_FIRST + SPREAD_STEP * r : P : 32, :].bitcast(I32),
+            )
+        w2_codes, w2_scale = quantise(w2_dealt, "w2", "x_scale_table")
+        e_codes = gather_words(e_table, e_list, "e_codes", "w2_dealt")
         w1_codes, w1_scale = quantise(w1_dealt, "w1", "e_table")
         x_codes = gather_words(x_table, x_list, "x_codes", "w1_dealt")
 
@@ -126,78 +133,78 @@ def tile_picked_yprimr_exp_p_kernel(
 
         for b in range(BANKS):
             i = b * BANK_STEPS // SLICE
-            first_product(b, w2_codes, w2_scale, e_codes[i], i * SLICE, e_scale[E_ROW:, :], True)
+            first_product(b, w2_codes, w2_scale, e_codes[i], i * SLICE, e_scale, True)
 
         def tanh_bank(b):
             i = b * BANK_STEPS // SLICE
-            first_product(b, w1_codes, w1_scale, x_codes[i], i * SLICE, x_scale, False)
+            first_product(b, w1_codes, w1_scale, x_codes[i], i * SLICE, x_scale[X_ROW:, :], False)
             nc.scalar.activation(
                 th[:, b * BANK_STEPS * PACK : (b + 1) * BANK_STEPS * PACK].rearrange("p (s t) -> p s t", t=PACK),
                 diff[b][:].rearrange("p (t s) -> p s t", t=PACK),
                 ACT.Tanh,
             )
 
-        starts = [sum(CHUNK_BANKS[:c]) * BANK_STEPS for c in range(len(CHUNK_BANKS))]
-        widths = [nb * BANK_STEPS for nb in CHUNK_BANKS]
-        nchunks = len(CHUNK_BANKS)
         two = sb([P, S * PACK], F32, "two")
         dcs = sb([P, S * PACK], F32, "dcs")
-        edges = [0] + [s - 1 for s in starts[1:]] + [S]
-        tot = [sb([P, n], F32, "tot%d" % c) for c, n in enumerate(widths)]
-        half = [sb([P, n], F32, "half%d" % c) for c, n in enumerate(widths)]
-        rest = [sb([P, n], F32, "rest%d" % c) for c, n in enumerate(widths)]
-        err = [sb([P, n], F32, "err%d" % c) for c, n in enumerate(widths)]
-        erru = [sb([P, n], F32, "erru%d" % c) for c, n in enumerate(widths)]
-        hid = [sb([P, n * PACK], BF16, "hid%d" % c) for c, n in enumerate(widths)]
-        hid_codes = [sb([P, n], U32, "hid_codes%d" % c) for c, n in enumerate(widths)]
-        hid_scale = [sb([P, n], U8, "hid_scale%d" % c) for c, n in enumerate(widths)]
+        tot = sb([P, V * PACK], F32, "tot")
+        half = sb([P, V * PACK], F32, "half")
+        rest = sb([P, V * PACK], F32, "rest")
+        err = sb([P, V * PACK], F32, "err")
+        erru = sb([P, V * PACK], F32, "erru")
+        hid = sb([P, S * PACK], BF16, "hid")
+        hid_codes = sb([P, S], U32, "hid_codes")
+        hid_scale = sb([P, S], U8, "hid_scale")
+        res = sb([P, S], F32, "res")
 
-        def pair_sums(c):
-            a, b = edges[c] * PACK, edges[c + 1] * PACK
+        def early(s0, s1):
+            return max(s0 - 1, 0) * PACK, (s1 if s1 == S else s1 - 1) * PACK
+
+        def by_step(tile, s0, s1):
+            return tile[:, s0 * PACK : s1 * PACK].rearrange("p (v d t) -> p v d t", d=D, t=PACK)
+
+        def by_answer(tile, s0, s1):
+            return tile[:, s0 // D * PACK : s1 // D * PACK].rearrange("p (v t) -> p v t", t=PACK)
+
+        def pair_sums(s0, s1):
+            a, b = early(s0, s1)
             nc.vector.tensor_tensor(two[:, a:b], th[:, a:b], th[:, a + PACK : b + PACK], ALU.add)
 
-        def steps_of(tile, c):
-            return tile[:, starts[c] * PACK : (starts[c] + widths[c]) * PACK].rearrange("p (v d t) -> p v d t", d=D, t=PACK)
+        def totals(s0, s1):
+            pairs = by_step(two, s0, s1)
+            nc.vector.tensor_tensor(by_answer(tot, s0, s1), pairs[:, :, 0, :], pairs[:, :, 2, :], ALU.add)
+            nc.scalar.activation(by_answer(half, s0, s1), by_answer(tot, s0, s1), ACT.Tanh, scale=0.4)
 
-        def totals(c):
-            pairs = steps_of(two, c)
-            nc.vector.tensor_tensor(
-                tot[c][:].rearrange("p (v t) -> p v t", t=PACK), pairs[:, :, 0, :], pairs[:, :, 2, :], ALU.add
-            )
-            nc.scalar.activation(half[c][:], tot[c][:], ACT.Tanh, scale=0.4)
-
-        def discounts(c):
-            a, b = edges[c] * PACK, edges[c + 1] * PACK
+        def discounts(s0, s1):
+            a, b = early(s0, s1)
             nc.scalar.activation(dcs[:, a:b], two[:, a:b], ACT.Exp, scale=-0.8)
 
-        def outcomes(c):
-            v0, nv = starts[c] // D, widths[c] // D
+        def outcomes(s0, s1):
             nc.scalar.activation(
-                rest[c][:].rearrange("p (v t) -> p v t", t=PACK),
-                lab_raw[:].rearrange("p (t v) -> p v t", t=PACK)[:, v0 : v0 + nv, :],
+                by_answer(rest, s0, s1),
+                lab_raw[:].rearrange("p (t v) -> p v t", t=PACK)[:, s0 // D : s1 // D, :],
                 ACT.Copy,
                 scale=-1.0,
                 bias=0.5,
             )
 
-        def errors(c):
-            nc.vector.scalar_tensor_tensor(err[c][:], half[c][:], 0.5, rest[c][:], ALU.mult, ALU.add)
+        def errors(s0, s1):
+            nc.vector.scalar_tensor_tensor(
+                by_answer(err, s0, s1), by_answer(half, s0, s1), 0.5, by_answer(rest, s0, s1), ALU.mult, ALU.add
+            )
 
-        def scaled_errors(c):
-            nv = widths[c] // D
+        def scaled_errors(s0, s1):
             nc.vector.tensor_tensor(
-                erru[c][:].rearrange("p (v t) -> p v t", t=PACK),
-                err[c][:].rearrange("p (v t) -> p v t", t=PACK),
-                unit_sb[:].unsqueeze(1).to_broadcast([P, nv, PACK]),
+                by_answer(erru, s0, s1),
+                by_answer(err, s0, s1),
+                unit_sb[:].unsqueeze(1).to_broadcast([P, (s1 - s0) // D, PACK]),
                 ALU.mult,
             )
 
-        def hidden(c):
-            nv = widths[c] // D
+        def hidden(s0, s1):
             nc.vector.tensor_tensor(
-                hid[c][:].rearrange("p (v d t) -> p v d t", d=D, t=PACK),
-                steps_of(dcs, c),
-                erru[c][:].rearrange("p (v t) -> p v t", t=PACK).unsqueeze(2).to_broadcast([P, nv, D, PACK]),
+                by_step(hid, s0, s1),
+                by_step(dcs, s0, s1),
+                by_answer(erru, s0, s1).unsqueeze(2).to_broadcast([P, (s1 - s0) // D, D, PACK]),
                 ALU.mult,
             )
 
@@ -213,44 +220,61 @@ def tile_picked_yprimr_exp_p_kernel(
             )
             nc.vector.quantize_mx(w3_codes[:].bitcast(FP8X4), w3_scale[:], w3_grouped[:])
 
-        def finish(c):
-            n = widths[c]
-            nc.vector.quantize_mx(hid_codes[c][:].bitcast(FP8X4), hid_scale[c][:], hid[c][:])
-            acc = psum.tile([P, PACK * BANK_STEPS], F32, name="acc%d" % c, tag="bank%d" % c)
+        def finish(s0, s1):
+            nc.vector.quantize_mx(
+                hid_codes[:, s0:s1].bitcast(FP8X4), hid_scale[:, s0:s1], hid[:, s0 * PACK : s1 * PACK]
+            )
+            acc = psum.tile([P, s1 - s0], F32, name="acc%d" % s0, tag="bank%d" % (s0 // BANK_STEPS))
             nc.tensor.matmul_mx(
-                acc[:, :n],
+                acc[:],
                 lhsT=w3_codes[:].bitcast(FP8X4),
                 lhsT_scale=w3_scale[:],
-                rhs=hid_codes[c][:].bitcast(FP8X4),
-                rhs_scale=hid_scale[c][:],
+                rhs=hid_codes[:, s0:s1].bitcast(FP8X4),
+                rhs_scale=hid_scale[:, s0:s1],
                 start=True,
                 stop=True,
             )
-            res = sb([P, n], F32, "res%d" % c)
-            nc.scalar.copy(res[:], acc[:, :n])
-            nc.sync.dma_start(out[:, starts[c] : starts[c] + n], res[:])
+            if s1 < S:
+                nc.scalar.copy(res[:, s0:s1], acc[:])
+            else:
+                nc.vector.tensor_copy(res[:, s0:s1], acc[:])
+            nc.sync.dma_start(out[:, s0:s1], res[:, s0:s1])
 
-        def tanh_chunk(c):
-            for b in range(starts[c] // BANK_STEPS, (starts[c] + widths[c]) // BANK_STEPS):
+        chunks = [(s0, s0 + CHUNK) for s0 in range(0, S, CHUNK)]
+        last = len(chunks) - 1
+
+        def halves(s0, s1):
+            return [(s0, (s0 + s1) // 2), ((s0 + s1) // 2, s1)]
+
+        def tanh_steps(s0, s1):
+            for b in range(s0 // BANK_STEPS, s1 // BANK_STEPS):
                 tanh_bank(b)
 
-        tanh_chunk(0)
-        for r in range(nchunks + 2):
-            if r < nchunks:
-                pair_sums(r)
-            if r + 1 < nchunks:
-                tanh_chunk(r + 1)
-            if 1 <= r <= nchunks:
-                errors(r - 1)
-            if r < nchunks:
-                totals(r)
-                outcomes(r)
-                discounts(r)
+        outcomes(*chunks[0])
+        for part in halves(*chunks[0]):
+            tanh_steps(*part)
+            pair_sums(*part)
+        for r in range(len(chunks) + 1):
+            if 1 <= r <= last:
+                pair_sums(*chunks[r])
+            if r < last:
+                tanh_steps(*chunks[r + 1])
+            if r >= 1:
+                errors(*chunks[r - 1])
+            if r <= last:
+                totals(*chunks[r])
+                if r >= 1:
+                    outcomes(*chunks[r])
+                discounts(*chunks[r])
             if r == 1:
                 quantise_w3()
             if r >= 2:
-                hidden(r - 2)
-            if 1 <= r <= nchunks:
-                scaled_errors(r - 1)
+                hidden(*chunks[r - 2])
+            if r >= 1:
+                scaled_errors(*chunks[r - 1])
             if r >= 2:
-                finish(r - 2)
+                finish(*chunks[r - 2])
+        for part in halves(*chunks[last]):
+            hidden(*part)
+        for part in halves(*chunks[last]):
+            finish(*part)

from contextlib import ExitStack

import concourse.mybir as mybir

K, T, W, S, D, N, H = 512, 4096, 2048, 1024, 4, 128, 512
V = S // D
FLOPS = 2 * (2 * K * H * S + H * N * S)

F32 = mybir.dt.float32
BF16 = mybir.dt.bfloat16
I32 = mybir.dt.int32
U32 = mybir.dt.uint32
U16 = mybir.dt.uint16
U8 = mybir.dt.uint8
FP8X4 = mybir.dt.float8_e4m3fn_x4
ACT = mybir.ActivationFunctionType
ALU = mybir.AluOpType

P = 128
PACK = 4
BANK_STEPS = 128
BANKS = S // BANK_STEPS
X_ROW = 8
SPREAD_FIRST, SPREAD_STEP = 4, 8
SLICE = 512
CHUNK = 256


def tile_picked_yprimr_exp_p_kernel(
    tc, x_words, x_scales, w1, e_words, e_scales, w2, lab, unit, w3, offs, rstp, out
):
    nc = tc.nc
    with ExitStack() as ctx:
        keep = ctx.enter_context(tc.tile_pool(name="keep", bufs=1))
        psum = ctx.enter_context(tc.psum_pool(name="psum", bufs=1))

        def sb(shape, dtype, name, tag=None):
            return keep.tile(shape, dtype, name=name, tag=tag or name, align_bytes=64)

        x_list = sb([P, S // 16], U16, "x_list")
        e_list = sb([P, S // 16], U16, "e_list")
        x_table = sb([P, T], U32, "x_table")
        e_table = sb([P, W], U32, "e_table")
        x_scale_table = sb([P, T], U8, "x_scale_table")
        e_scale_table = sb([P, W], U8, "e_scale_table")
        w1_raw = sb([P, PACK * H], F32, "w1_raw")
        w2_raw = sb([P, PACK * H], F32, "w2_raw")
        w3_raw = sb([P, PACK * N], F32, "w3_raw")
        lab_raw = sb([P, PACK * V], F32, "lab_raw")
        unit_sb = sb([P, PACK], F32, "unit_sb")

        th = sb([P, (S + 1) * PACK], F32, "th")
        past_end = sb([P, PACK], F32, "past_end")

        nc.gpsimd.memset(e_scale_table[:].bitcast(I32), 0)
        nc.vector.memset(x_scale_table[:].bitcast(I32), 0)
        nc.gpsimd.memset(past_end[:], 0.0)
        x_scale = sb([P, S], U8, "x_scale")
        nc.gpsimd.memset(x_scale[:].bitcast(I32), 0)
        nc.scalar.activation(th[:, S * PACK :], past_end[:], ACT.Tanh)
        w2_rows = w2.rearrange("(p j) c -> p (j c)", j=PACK)
        nc.sync.dma_start(e_list[:], rstp)
        nc.sync.dma_start(w2_raw[:, : 2 * H], w2_rows[:, : 2 * H])
        nc.sync.dma_start(x_list[:], offs)
        nc.sync.dma_start(w2_raw[:, 2 * H :], w2_rows[:, 2 * H :])
        for r in range(4):
            nc.sync.dma_start(e_scale_table[r:P:32, :].bitcast(I32), e_scales[0][r:16:4, :].bitcast(I32))
        nc.sync.dma_start(w1_raw[:], w1.rearrange("(p j) c -> p (j c)", j=PACK))
        nc.sync.dma_start(x_scale_table[SPREAD_FIRST:P:SPREAD_STEP, :].bitcast(I32), x_scales[0].bitcast(I32))
        nc.sync.dma_start(e_table[:].bitcast(I32), e_words[0].rearrange("p n r -> p (n r)").bitcast(I32))
        nc.sync.dma_start(x_table[:].bitcast(I32), x_words[0].rearrange("p n r -> p (n r)").bitcast(I32))
        nc.sync.dma_start(lab_raw[:], lab.rearrange("(p t) v -> p (t v)", t=PACK))
        nc.sync.dma_start(unit_sb[:], unit.rearrange("(p t) o -> p (t o)", t=PACK))
        nc.sync.dma_start(w3_raw[:], w3.rearrange("(p t) m -> p (t m)", t=PACK))

        def deal(raw, sign, name):
            dealt = sb([P, PACK * H], BF16, name)
            nc.scalar.activation(
                dealt[:].rearrange("p (t m j) -> p m t j", t=PACK, j=PACK),
                raw[:].rearrange("p (j m t) -> p m t j", j=PACK, t=PACK),
                ACT.Copy,
                scale=sign,
            )
            return dealt

        def quantise(dealt, name, tag):
            codes = sb([P, H], U32, name + "_codes", tag)
            scale = sb([P, H], U8, name + "_scale")
            nc.vector.quantize_mx(codes[:].bitcast(FP8X4), scale[:], dealt[:])
            return codes, scale

        def gather_words(table, entries, name, first_tag):
            pieces = []
            for s0 in range(0, S, SLICE):
                picked = sb([P, SLICE], U32, name + str(s0), first_tag if s0 == 0 else None)
                nc.vector.tensor_copy(picked[:], table[:].indirect(entries[:, s0 // 16 : (s0 + SLICE) // 16]))
                pieces.append(picked)
            return pieces

        w2_dealt = deal(w2_raw, -1.0, "w2_dealt")
        w1_dealt = deal(w1_raw, 1.0, "w1_dealt")

        e_scale = sb([P, S], U8, "e_scale")
        nc.vector.tensor_copy(e_scale[:], e_scale_table[:].indirect(e_list[:]))
        x_spread = sb([P, S], U8, "x_spread", "e_scale_table")
        nc.vector.tensor_copy(x_spread[:], x_scale_table[:].indirect(x_list[:]))
        for r in range(4):
            nc.scalar.dma_start(
                x_scale[X_ROW + r : P : 32, :].bitcast(I32),
                x_spread[SPREAD_FIRST + SPREAD_STEP * r : P : 32, :].bitcast(I32),
            )
        w2_codes, w2_scale = quantise(w2_dealt, "w2", "x_scale_table")
        e_codes = gather_words(e_table, e_list, "e_codes", "w2_dealt")
        w1_codes, w1_scale = quantise(w1_dealt, "w1", "e_table")
        x_codes = gather_words(x_table, x_list, "x_codes", "w1_dealt")

        diff = [psum.tile([P, PACK * BANK_STEPS], F32, name="diff%d" % b, tag="bank%d" % b) for b in range(BANKS)]

        def first_product(bank, w_codes, w_scale, codes, col0, scale, opens):
            steps = slice(bank * BANK_STEPS, (bank + 1) * BANK_STEPS)
            local = slice(steps.start - col0, steps.stop - col0)
            for t in range(PACK):
                cols = slice(t * P, (t + 1) * P)
                nc.tensor.matmul_mx(
                    diff[bank][:, t * BANK_STEPS : (t + 1) * BANK_STEPS],
                    lhsT=w_codes[:, cols].bitcast(FP8X4),
                    lhsT_scale=w_scale[:, cols],
                    rhs=codes[:, local].bitcast(FP8X4),
                    rhs_scale=scale[:, steps],
                    start=(opens and t == 0),
                    stop=(not opens and t == PACK - 1),
                )

        for b in range(BANKS):
            i = b * BANK_STEPS // SLICE
            first_product(b, w2_codes, w2_scale, e_codes[i], i * SLICE, e_scale, True)

        def tanh_bank(b):
            i = b * BANK_STEPS // SLICE
            first_product(b, w1_codes, w1_scale, x_codes[i], i * SLICE, x_scale[X_ROW:, :], False)
            nc.scalar.activation(
                th[:, b * BANK_STEPS * PACK : (b + 1) * BANK_STEPS * PACK].rearrange("p (s t) -> p s t", t=PACK),
                diff[b][:].rearrange("p (t s) -> p s t", t=PACK),
                ACT.Tanh,
            )

        two = sb([P, S * PACK], F32, "two")
        dcs = sb([P, S * PACK], F32, "dcs")
        tot = sb([P, V * PACK], F32, "tot")
        half = sb([P, V * PACK], F32, "half")
        rest = sb([P, V * PACK], F32, "rest")
        err = sb([P, V * PACK], F32, "err")
        erru = sb([P, V * PACK], F32, "erru")
        hid = sb([P, S * PACK], BF16, "hid")
        hid_codes = sb([P, S], U32, "hid_codes")
        hid_scale = sb([P, S], U8, "hid_scale")
        res = sb([P, S], F32, "res")

        def early(s0, s1):
            return max(s0 - 1, 0) * PACK, (s1 if s1 == S else s1 - 1) * PACK

        def by_step(tile, s0, s1):
            return tile[:, s0 * PACK : s1 * PACK].rearrange("p (v d t) -> p v d t", d=D, t=PACK)

        def by_answer(tile, s0, s1):
            return tile[:, s0 // D * PACK : s1 // D * PACK].rearrange("p (v t) -> p v t", t=PACK)

        def pair_sums(s0, s1):
            a, b = early(s0, s1)
            nc.vector.tensor_tensor(two[:, a:b], th[:, a:b], th[:, a + PACK : b + PACK], ALU.add)

        def totals(s0, s1):
            pairs = by_step(two, s0, s1)
            nc.vector.tensor_tensor(by_answer(tot, s0, s1), pairs[:, :, 0, :], pairs[:, :, 2, :], ALU.add)
            nc.scalar.activation(by_answer(half, s0, s1), by_answer(tot, s0, s1), ACT.Tanh, scale=0.4)

        def discounts(s0, s1):
            a, b = early(s0, s1)
            nc.scalar.activation(dcs[:, a:b], two[:, a:b], ACT.Exp, scale=-0.8)

        def outcomes(s0, s1):
            nc.scalar.activation(
                by_answer(rest, s0, s1),
                lab_raw[:].rearrange("p (t v) -> p v t", t=PACK)[:, s0 // D : s1 // D, :],
                ACT.Copy,
                scale=-1.0,
                bias=0.5,
            )

        def errors(s0, s1):
            nc.vector.scalar_tensor_tensor(
                by_answer(err, s0, s1), by_answer(half, s0, s1), 0.5, by_answer(rest, s0, s1), ALU.mult, ALU.add
            )

        def scaled_errors(s0, s1):
            nc.vector.tensor_tensor(
                by_answer(erru, s0, s1),
                by_answer(err, s0, s1),
                unit_sb[:].unsqueeze(1).to_broadcast([P, (s1 - s0) // D, PACK]),
                ALU.mult,
            )

        def hidden(s0, s1):
            nc.vector.tensor_tensor(
                by_step(hid, s0, s1),
                by_step(dcs, s0, s1),
                by_answer(erru, s0, s1).unsqueeze(2).to_broadcast([P, (s1 - s0) // D, D, PACK]),
                ALU.mult,
            )

        w3_grouped = sb([P, PACK * N], BF16, "w3_grouped")
        w3_codes = sb([P, N], U32, "w3_codes")
        w3_scale = sb([P, N], U8, "w3_scale")

        def quantise_w3():
            nc.scalar.activation(
                w3_grouped[:].rearrange("p (m t) -> p m t", t=PACK),
                w3_raw[:].rearrange("p (t m) -> p m t", t=PACK),
                ACT.Copy,
            )
            nc.vector.quantize_mx(w3_codes[:].bitcast(FP8X4), w3_scale[:], w3_grouped[:])

        def finish(s0, s1):
            nc.vector.quantize_mx(
                hid_codes[:, s0:s1].bitcast(FP8X4), hid_scale[:, s0:s1], hid[:, s0 * PACK : s1 * PACK]
            )
            acc = psum.tile([P, s1 - s0], F32, name="acc%d" % s0, tag="bank%d" % (s0 // BANK_STEPS))
            nc.tensor.matmul_mx(
                acc[:],
                lhsT=w3_codes[:].bitcast(FP8X4),
                lhsT_scale=w3_scale[:],
                rhs=hid_codes[:, s0:s1].bitcast(FP8X4),
                rhs_scale=hid_scale[:, s0:s1],
                start=True,
                stop=True,
            )
            if s1 < S:
                nc.scalar.copy(res[:, s0:s1], acc[:])
            else:
                nc.vector.tensor_copy(res[:, s0:s1], acc[:])
            nc.sync.dma_start(out[:, s0:s1], res[:, s0:s1])

        chunks = [(s0, s0 + CHUNK) for s0 in range(0, S, CHUNK)]
        last = len(chunks) - 1

        def halves(s0, s1):
            return [(s0, (s0 + s1) // 2), ((s0 + s1) // 2, s1)]

        def tanh_steps(s0, s1):
            for b in range(s0 // BANK_STEPS, s1 // BANK_STEPS):
                tanh_bank(b)

        outcomes(*chunks[0])
        for part in halves(*chunks[0]):
            tanh_steps(*part)
            pair_sums(*part)
        for r in range(len(chunks) + 1):
            if 1 <= r <= last:
                pair_sums(*chunks[r])
            if r < last:
                tanh_steps(*chunks[r + 1])
            if r >= 1:
                errors(*chunks[r - 1])
            if r <= last:
                totals(*chunks[r])
                if r >= 1:
                    outcomes(*chunks[r])
                discounts(*chunks[r])
            if r == 1:
                quantise_w3()
            if r >= 2:
                hidden(*chunks[r - 2])
            if r >= 1:
                scaled_errors(*chunks[r - 1])
            if r >= 2:
                finish(*chunks[r - 2])
        for part in halves(*chunks[last]):
            hidden(*part)
        for part in halves(*chunks[last]):
            finish(*part)
